import numpy as np
CORES = [40,168,296,424]
N = 4
def setup_inputs(rng):
    return {"x": rng.standard_normal((N, 128, 256), dtype=np.float32)}
def reference(x):
    g = np.concatenate(list(x), axis=1)
    return {"y": np.broadcast_to(g, (N,) + g.shape)}

@@ -1,0 +1,75 @@
+from concourse.bass import DstId, RemoteDMATransfer
+W = 256
+K = 4
+C = 2
+R = 128 // K
+SCRATCH = {'land': ('dram', [4 * K, 128, W // K], 'float32')}
+SEMAPHORES = ['sent', 'relay', 'spread', 'l_first', 'l_rest', 'r_first', 'r_rest', 'stored', 'loaded0', 'loaded1', 'diag0', 'diag1']
+OFF_CHIP, ON_CHIP = (255, 65280)
+TO_NXT, TO_PRV = (15, 240)
+SPREAD_NXT, SPREAD_PRV = (3840, 61440)
+SWITCH_RELAYS, SWITCH_SPREADER = ((6, 7), 5)
+CABLE_RELAYS, CABLE_SPREADER = ((2, 3), 4)
+
+def by_switch(q, up):
+    return (q % 2 == 0) == up
+
+def relay(T, q, up, i):
+    return T.cores[q] + (SWITCH_RELAYS if by_switch(q, up) else CABLE_RELAYS)[i]
+
+def spreader(T, q, up):
+    return T.cores[q] + (SWITCH_SPREADER if by_switch(q, up) else CABLE_SPREADER)
+
+def rank_program(g, core, T, topo):
+    S = T.sem
+    loaded = [S.loaded0, S.loaded1]
+    diag = [S.diag0, S.diag1]
+
+    def tr(j, c, dst, mask, sem):
+        rid, pid = topo.addr(dst, core)
+        return RemoteDMATransfer(dst_ids=[DstId(rid=rid, pnc=pid)], dma_engine_mask=mask, remote_sem=sem, src=T.land[K * j + c], dst=T.land[K * j + c])
+    r = T.rank_of(core)
+    if r is None:
+        q = T.rank_of(core - core % 8)
+        if q is None:
+            return
+        for up in (True, False):
+            far = T.cores[(q + 1) % 4] if up else T.cores[(q - 1) % 4]
+            for i in range(C):
+                if core == relay(T, q, up, i):
+                    j, c = ((q - 1) % 4, 2 * i) if up else ((q + 1) % 4, 2 * i + 1)
+                    g.wait_ge(S.relay, 4)
+                    g.remote_dma_fused([tr(j, c, far, OFF_CHIP, diag[i]), tr(j, c, T.cores[q], ON_CHIP, S.l_first if up else S.r_first)], local_sem=S.sent)
+                    g.wait_ge(S.sent, 16)
+            if core == spreader(T, q, up):
+                g.wait_ge(S.spread, 4)
+                g.remote_dma_fused([tr(q, 1 if up else 0, far, OFF_CHIP, S.l_rest if up else S.r_rest)], local_sem=S.sent)
+                g.wait_ge(S.sent, 8)
+        return
+    left, right, d = ((r - 1) % 4, (r + 1) % 4, (r + 2) % 4)
+    nxt, prv = (T.cores[right], T.cores[left])
+
+    def store_block(j):
+        g.dma_start(T.y[:, W * j:W * (j + 1)], T.land[K * j:K * (j + 1)]).then_inc(S.stored, 16)
+
+    def store_diag(i):
+        g.wait_ge(diag[i], 16)
+        g.dma_start(T.y[2 * i * R:(2 * i + 2) * R, W * d:W * (d + 1)], T.land[K * d + 2 * i:K * d + 2 * i + 2]).then_inc(S.stored, 16)
+    for i in range(C):
+        g.dma_start(T.land[K * r + 2 * i:K * r + 2 * i + 2], T.x[2 * i * R:(2 * i + 2) * R, :]).then_inc(loaded[i], 16)
+    g.wait_ge(loaded[0], 16)
+    g.remote_dma_fused([tr(r, 0, relay(T, right, True, 0), TO_NXT, S.relay), tr(r, 1, relay(T, left, False, 0), TO_PRV, S.relay), tr(r, 1, spreader(T, r, True), SPREAD_NXT, S.spread), tr(r, 0, spreader(T, r, False), SPREAD_PRV, S.spread)], local_sem=S.sent)
+    g.wait_ge(loaded[1], 16)
+    g.remote_dma_fused([tr(r, 2, relay(T, right, True, 1), TO_NXT, S.relay), tr(r, 3, relay(T, left, False, 1), TO_PRV, S.relay)], local_sem=S.sent)
+    g.remote_dma_fused([tr(r, 3, nxt, TO_NXT, S.l_rest), tr(r, 2, prv, TO_PRV, S.r_rest)], local_sem=S.sent)
+    g.dma_start(T.y[:, W * r:W * (r + 1)], T.x[:, :]).then_inc(S.stored, 16)
+    store_diag(0)
+    g.wait_ge(S.l_rest, 12)
+    g.wait_ge(S.l_first, 16)
+    store_block(left)
+    g.wait_ge(S.r_rest, 12)
+    g.wait_ge(S.r_first, 16)
+    store_block(right)
+    store_diag(1)
+    g.wait_ge(S.sent, 32)
+    g.wait_ge(S.stored, 80)

@@ -1,33 +1,34 @@
 from concourse.bass import DstId, RemoteDMATransfer
+
 W = 256
 K = 4
-C = 2
 R = 128 // K
 SCRATCH = {'land': ('dram', [4 * K, 128, W // K], 'float32')}
-SEMAPHORES = ['sent', 'relay', 'spread', 'l_first', 'l_rest', 'r_first', 'r_rest', 'stored', 'loaded0', 'loaded1', 'diag0', 'diag1']
-OFF_CHIP, ON_CHIP = (255, 65280)
-TO_NXT, TO_PRV = (15, 240)
-SPREAD_NXT, SPREAD_PRV = (3840, 61440)
-SWITCH_RELAYS, SWITCH_SPREADER = ((6, 7), 5)
-CABLE_RELAYS, CABLE_SPREADER = ((2, 3), 4)
+SEMAPHORES = ['loaded', 'sent', 'relay', 'spread', 'L', 'Rt', 'D', 'stored']
+SWITCH_RELAYS, SWITCH_SPREADERS = (5, 7), (3, 3)
+CABLE_RELAYS, CABLE_SPREADERS = (2, 4), (1, 6)
+
 
 def by_switch(q, up):
     return (q % 2 == 0) == up
 
+
 def relay(T, q, up, i):
     return T.cores[q] + (SWITCH_RELAYS if by_switch(q, up) else CABLE_RELAYS)[i]
 
-def spreader(T, q, up):
-    return T.cores[q] + (SWITCH_SPREADER if by_switch(q, up) else CABLE_SPREADER)
+
+def spreader(T, q, up, i):
+    return T.cores[q] + (SWITCH_SPREADERS if by_switch(q, up) else CABLE_SPREADERS)[i]
+
 
 def rank_program(g, core, T, topo):
     S = T.sem
-    loaded = [S.loaded0, S.loaded1]
-    diag = [S.diag0, S.diag1]
 
     def tr(j, c, dst, mask, sem):
         rid, pid = topo.addr(dst, core)
-        return RemoteDMATransfer(dst_ids=[DstId(rid=rid, pnc=pid)], dma_engine_mask=mask, remote_sem=sem, src=T.land[K * j + c], dst=T.land[K * j + c])
+        return RemoteDMATransfer(dst_ids=[DstId(rid=rid, pnc=pid)], dma_engine_mask=mask, remote_sem=sem,
+                                 src=T.land[K * j + c], dst=T.land[K * j + c])
+
     r = T.rank_of(core)
     if r is None:
         q = T.rank_of(core - core % 8)
@@ -35,41 +36,51 @@ def rank_program(g, core, T, topo):
             return
         for up in (True, False):
             far = T.cores[(q + 1) % 4] if up else T.cores[(q - 1) % 4]
-            for i in range(C):
+            for i in range(2):
                 if core == relay(T, q, up, i):
                     j, c = ((q - 1) % 4, 2 * i) if up else ((q + 1) % 4, 2 * i + 1)
-                    g.wait_ge(S.relay, 4)
-                    g.remote_dma_fused([tr(j, c, far, OFF_CHIP, diag[i]), tr(j, c, T.cores[q], ON_CHIP, S.l_first if up else S.r_first)], local_sem=S.sent)
+                    g.wait_ge(S.relay, 2)
+                    g.remote_dma_fused([tr(j, c, far, 0x00FF, S.D),
+                                        tr(j, c, T.cores[q], 0xFF00, S.L if up else S.Rt)], local_sem=S.sent)
                     g.wait_ge(S.sent, 16)
-            if core == spreader(T, q, up):
-                g.wait_ge(S.spread, 4)
-                g.remote_dma_fused([tr(q, 1 if up else 0, far, OFF_CHIP, S.l_rest if up else S.r_rest)], local_sem=S.sent)
+            mine = [i for i in range(2) if core == spreader(T, q, up, i)]
+            if mine:
+                sem = S.L if up else S.Rt
+                g.wait_ge(S.spread, 2 * len(mine))
+                masks = [0x00FF] if len(mine) == 1 else [0x000F, 0x00F0]
+                g.remote_dma_fused([tr(q, 2 * i + (1 if up else 0), far, m, sem) for i, m in zip(mine, masks)],
+                                   local_sem=S.sent)
                 g.wait_ge(S.sent, 8)
         return
-    left, right, d = ((r - 1) % 4, (r + 1) % 4, (r + 2) % 4)
-    nxt, prv = (T.cores[right], T.cores[left])
 
-    def store_block(j):
-        g.dma_start(T.y[:, W * j:W * (j + 1)], T.land[K * j:K * (j + 1)]).then_inc(S.stored, 16)
+    left, right, d = (r - 1) % 4, (r + 1) % 4, (r + 2) % 4
+    g.sync.dma_start(T.land[K * r:K * (r + 1)], T.x[:, :]).then_inc(S.loaded, 16)
+    g.wait_ge(S.loaded, 16)
+    g.remote_dma_fused([
+        tr(r, 0, relay(T, right, True, 0), 0x0003, S.relay),
+        tr(r, 2, relay(T, right, True, 1), 0x000C, S.relay),
+        tr(r, 1, relay(T, left, False, 0), 0x0030, S.relay),
+        tr(r, 3, relay(T, left, False, 1), 0x00C0, S.relay),
+        tr(r, 1, spreader(T, r, True, 0), 0x0300, S.spread),
+        tr(r, 3, spreader(T, r, True, 1), 0x0C00, S.spread),
+        tr(r, 0, spreader(T, r, False, 0), 0x3000, S.spread),
+        tr(r, 2, spreader(T, r, False, 1), 0xC000, S.spread)], local_sem=S.sent)
 
-    def store_diag(i):
-        g.wait_ge(diag[i], 16)
-        g.dma_start(T.y[2 * i * R:(2 * i + 2) * R, W * d:W * (d + 1)], T.land[K * d + 2 * i:K * d + 2 * i + 2]).then_inc(S.stored, 16)
-    for i in range(C):
-        g.dma_start(T.land[K * r + 2 * i:K * r + 2 * i + 2], T.x[2 * i * R:(2 * i + 2) * R, :]).then_inc(loaded[i], 16)
-    g.wait_ge(loaded[0], 16)
-    g.remote_dma_fused([tr(r, 0, relay(T, right, True, 0), TO_NXT, S.relay), tr(r, 1, relay(T, left, False, 0), TO_PRV, S.relay), tr(r, 1, spreader(T, r, True), SPREAD_NXT, S.spread), tr(r, 0, spreader(T, r, False), SPREAD_PRV, S.spread)], local_sem=S.sent)
-    g.wait_ge(loaded[1], 16)
-    g.remote_dma_fused([tr(r, 2, relay(T, right, True, 1), TO_NXT, S.relay), tr(r, 3, relay(T, left, False, 1), TO_PRV, S.relay)], local_sem=S.sent)
-    g.remote_dma_fused([tr(r, 3, nxt, TO_NXT, S.l_rest), tr(r, 2, prv, TO_PRV, S.r_rest)], local_sem=S.sent)
-    g.dma_start(T.y[:, W * r:W * (r + 1)], T.x[:, :]).then_inc(S.stored, 16)
-    store_diag(0)
-    g.wait_ge(S.l_rest, 12)
-    g.wait_ge(S.l_first, 16)
-    store_block(left)
-    g.wait_ge(S.r_rest, 12)
-    g.wait_ge(S.r_first, 16)
-    store_block(right)
-    store_diag(1)
-    g.wait_ge(S.sent, 32)
+    n_l = 16 + (8 if by_switch(left, True) else 16)
+    n_r = 16 + (8 if by_switch(right, False) else 16)
+
+    def store(qu, j, lo, hi):
+        qu.dma_start(T.y[lo * R:hi * R, W * j:W * (j + 1)], T.land[K * j + lo:K * j + hi]).then_inc(S.stored, 16)
+
+    g.scalar.wait_ge(S.sent, 16)
+    g.scalar.dma_start(T.y[:, W * r:W * (r + 1)], T.x[:, :]).then_inc(S.stored, 16)
+    g.sync.wait_ge(S.L, n_l)
+    store(g.sync, left, 0, K)
+    g.scalar.wait_ge(S.Rt, n_r)
+    store(g.scalar, right, 0, K)
+    g.sync.wait_ge(S.D, 32)
+    store(g.sync, d, 0, 2)
+    g.scalar.wait_ge(S.D, 32)
+    store(g.scalar, d, 2, 4)
+    g.wait_ge(S.sent, 16)
     g.wait_ge(S.stored, 80)

@@ -4,9 +4,9 @@ W = 256
 K = 4
 R = 128 // K
 SCRATCH = {'land': ('dram', [4 * K, 128, W // K], 'float32')}
-SEMAPHORES = ['loaded', 'sent', 'relay', 'spread', 'L', 'Rt', 'D', 'stored']
-SWITCH_RELAYS, SWITCH_SPREADERS = (5, 7), (3, 3)
-CABLE_RELAYS, CABLE_SPREADERS = (2, 4), (1, 6)
+SEMAPHORES = ['loaded', 'sent', 'relay', 'spread', 'Ls', 'Lr', 'Rs', 'Rr', 'Da', 'Db', 'stored', 'own']
+SWITCH_RELAYS, SWITCH_SPREADERS = (3, 5), (7, 7)
+CABLE_RELAYS, CABLE_SPREADERS = (1, 2), (4, 6)
 
 
 def by_switch(q, up):
@@ -38,17 +38,17 @@ def rank_program(g, core, T, topo):
             far = T.cores[(q + 1) % 4] if up else T.cores[(q - 1) % 4]
             for i in range(2):
                 if core == relay(T, q, up, i):
-                    j, c = ((q - 1) % 4, 2 * i) if up else ((q + 1) % 4, 2 * i + 1)
+                    j, c = ((q - 1) % 4, i) if up else ((q + 1) % 4, 2 + i)
                     g.wait_ge(S.relay, 2)
-                    g.remote_dma_fused([tr(j, c, far, 0x00FF, S.D),
-                                        tr(j, c, T.cores[q], 0xFF00, S.L if up else S.Rt)], local_sem=S.sent)
+                    g.remote_dma_fused([tr(j, c, far, 0x00FF, S.Da if up else S.Db),
+                                        tr(j, c, T.cores[q], 0xFF00, S.Lr if up else S.Rr)], local_sem=S.sent)
                     g.wait_ge(S.sent, 16)
             mine = [i for i in range(2) if core == spreader(T, q, up, i)]
             if mine:
-                sem = S.L if up else S.Rt
+                sem = S.Ls if up else S.Rs
                 g.wait_ge(S.spread, 2 * len(mine))
                 masks = [0x00FF] if len(mine) == 1 else [0x000F, 0x00F0]
-                g.remote_dma_fused([tr(q, 2 * i + (1 if up else 0), far, m, sem) for i, m in zip(mine, masks)],
+                g.remote_dma_fused([tr(q, i + (2 if up else 0), far, m, sem) for i, m in zip(mine, masks)],
                                    local_sem=S.sent)
                 g.wait_ge(S.sent, 8)
         return
@@ -58,29 +58,28 @@ def rank_program(g, core, T, topo):
     g.wait_ge(S.loaded, 16)
     g.remote_dma_fused([
         tr(r, 0, relay(T, right, True, 0), 0x0003, S.relay),
-        tr(r, 2, relay(T, right, True, 1), 0x000C, S.relay),
-        tr(r, 1, relay(T, left, False, 0), 0x0030, S.relay),
+        tr(r, 1, relay(T, right, True, 1), 0x000C, S.relay),
+        tr(r, 2, relay(T, left, False, 0), 0x0030, S.relay),
         tr(r, 3, relay(T, left, False, 1), 0x00C0, S.relay),
-        tr(r, 1, spreader(T, r, True, 0), 0x0300, S.spread),
+        tr(r, 2, spreader(T, r, True, 0), 0x0300, S.spread),
         tr(r, 3, spreader(T, r, True, 1), 0x0C00, S.spread),
         tr(r, 0, spreader(T, r, False, 0), 0x3000, S.spread),
-        tr(r, 2, spreader(T, r, False, 1), 0xC000, S.spread)], local_sem=S.sent)
+        tr(r, 1, spreader(T, r, False, 1), 0xC000, S.spread)], local_sem=S.sent)
 
-    n_l = 16 + (8 if by_switch(left, True) else 16)
-    n_r = 16 + (8 if by_switch(right, False) else 16)
+    n_ls = 8 if by_switch(left, True) else 16
+    n_rs = 8 if by_switch(right, False) else 16
 
-    def store(qu, j, lo, hi):
+    def store(qu, sem, n, j, lo, hi):
+        qu.wait_ge(sem, n)
         qu.dma_start(T.y[lo * R:hi * R, W * j:W * (j + 1)], T.land[K * j + lo:K * j + hi]).then_inc(S.stored, 16)
 
-    g.scalar.wait_ge(S.sent, 16)
-    g.scalar.dma_start(T.y[:, W * r:W * (r + 1)], T.x[:, :]).then_inc(S.stored, 16)
-    g.sync.wait_ge(S.L, n_l)
-    store(g.sync, left, 0, K)
-    g.scalar.wait_ge(S.Rt, n_r)
-    store(g.scalar, right, 0, K)
-    g.sync.wait_ge(S.D, 32)
-    store(g.sync, d, 0, 2)
-    g.scalar.wait_ge(S.D, 32)
-    store(g.scalar, d, 2, 4)
+    store(g.sync, S.Ls, n_ls, left, 2, 4)
+    store(g.scalar, S.Rs, n_rs, right, 0, 2)
+    store(g.sync, S.Lr, 16, left, 0, 2)
+    store(g.scalar, S.Rr, 16, right, 2, 4)
+    store(g.sync, S.Da, 16, d, 0, 2)
+    store(g.scalar, S.Db, 16, d, 2, 4)
     g.wait_ge(S.sent, 16)
-    g.wait_ge(S.stored, 80)
+    g.dma_start(T.y[:, W * r:W * (r + 1)], T.x[:, :]).then_inc(S.own, 16)
+    g.wait_ge(S.own, 16)
+    g.wait_ge(S.stored, 96)

@@ -4,21 +4,9 @@ W = 256
 K = 4
 R = 128 // K
 SCRATCH = {'land': ('dram', [4 * K, 128, W // K], 'float32')}
-SEMAPHORES = ['loaded', 'sent', 'relay', 'spread', 'Ls', 'Lr', 'Rs', 'Rr', 'Da', 'Db', 'stored', 'own']
-SWITCH_RELAYS, SWITCH_SPREADERS = (3, 5), (7, 7)
-CABLE_RELAYS, CABLE_SPREADERS = (1, 2), (4, 6)
-
-
-def by_switch(q, up):
-    return (q % 2 == 0) == up
-
-
-def relay(T, q, up, i):
-    return T.cores[q] + (SWITCH_RELAYS if by_switch(q, up) else CABLE_RELAYS)[i]
-
-
-def spreader(T, q, up, i):
-    return T.cores[q] + (SWITCH_SPREADERS if by_switch(q, up) else CABLE_SPREADERS)[i]
+SEMAPHORES = ['loaded', 'sent', 'relay', 'spread', 'Sw', 'Cb', 'D', 'stored']
+SENDER = (0, 4, 2, 6)
+RELAY = (1, 5, 3, 7)
 
 
 def rank_program(g, core, T, topo):
@@ -29,57 +17,45 @@ def rank_program(g, core, T, topo):
         return RemoteDMATransfer(dst_ids=[DstId(rid=rid, pnc=pid)], dma_engine_mask=mask, remote_sem=sem,
                                  src=T.land[K * j + c], dst=T.land[K * j + c])
 
-    r = T.rank_of(core)
-    if r is None:
-        q = T.rank_of(core - core % 8)
-        if q is None:
-            return
-        for up in (True, False):
-            far = T.cores[(q + 1) % 4] if up else T.cores[(q - 1) % 4]
-            for i in range(2):
-                if core == relay(T, q, up, i):
-                    j, c = ((q - 1) % 4, i) if up else ((q + 1) % 4, 2 + i)
-                    g.wait_ge(S.relay, 2)
-                    g.remote_dma_fused([tr(j, c, far, 0x00FF, S.Da if up else S.Db),
-                                        tr(j, c, T.cores[q], 0xFF00, S.Lr if up else S.Rr)], local_sem=S.sent)
-                    g.wait_ge(S.sent, 16)
-            mine = [i for i in range(2) if core == spreader(T, q, up, i)]
-            if mine:
-                sem = S.Ls if up else S.Rs
-                g.wait_ge(S.spread, 2 * len(mine))
-                masks = [0x00FF] if len(mine) == 1 else [0x000F, 0x00F0]
-                g.remote_dma_fused([tr(q, i + (2 if up else 0), far, m, sem) for i, m in zip(mine, masks)],
-                                   local_sem=S.sent)
-                g.wait_ge(S.sent, 8)
+    q = T.rank_of(core - core % 8)
+    if q is None:
+        return
+    sw, cb, d = q ^ 1, 3 - q, (q + 2) % 4
+    me = core % 8
+
+    def send_out(c):
+        g.remote_dma_fused([tr(q, c, T.cores[cb] + RELAY[c], 0x000F, S.relay),
+                            tr(q, c, T.cores[sw], 0x00F0, S.Sw)], local_sem=S.sent)
+
+    if me != 0:
+        if me in SENDER:
+            g.wait_ge(S.spread, 2)
+            send_out(SENDER.index(me))
+            g.wait_ge(S.sent, 8)
+        else:
+            c = RELAY.index(me)
+            g.wait_ge(S.relay, 4)
+            g.remote_dma_fused([tr(cb, c, T.cores[sw], 0x00FF, S.D),
+                                tr(cb, c, T.cores[q], 0xFF00, S.Cb)], local_sem=S.sent)
+            g.wait_ge(S.sent, 16)
         return
 
-    left, right, d = (r - 1) % 4, (r + 1) % 4, (r + 2) % 4
-    g.sync.dma_start(T.land[K * r:K * (r + 1)], T.x[:, :]).then_inc(S.loaded, 16)
+    g.sync.dma_start(T.land[K * q:K * (q + 1)], T.x[:, :]).then_inc(S.loaded, 16)
     g.wait_ge(S.loaded, 16)
-    g.remote_dma_fused([
-        tr(r, 0, relay(T, right, True, 0), 0x0003, S.relay),
-        tr(r, 1, relay(T, right, True, 1), 0x000C, S.relay),
-        tr(r, 2, relay(T, left, False, 0), 0x0030, S.relay),
-        tr(r, 3, relay(T, left, False, 1), 0x00C0, S.relay),
-        tr(r, 2, spreader(T, r, True, 0), 0x0300, S.spread),
-        tr(r, 3, spreader(T, r, True, 1), 0x0C00, S.spread),
-        tr(r, 0, spreader(T, r, False, 0), 0x3000, S.spread),
-        tr(r, 1, spreader(T, r, False, 1), 0xC000, S.spread)], local_sem=S.sent)
+    g.remote_dma_fused([tr(q, 0, T.cores[cb] + RELAY[0], 0x000F, S.relay),
+                        tr(q, 0, T.cores[sw], 0x00F0, S.Sw),
+                        tr(q, 1, core + SENDER[1], 0x0300, S.spread),
+                        tr(q, 2, core + SENDER[2], 0x0C00, S.spread),
+                        tr(q, 3, core + SENDER[3], 0x3000, S.spread)], local_sem=S.sent)
 
-    n_ls = 8 if by_switch(left, True) else 16
-    n_rs = 8 if by_switch(right, False) else 16
-
-    def store(qu, sem, n, j, lo, hi):
+    def store(qu, sem, n, j):
         qu.wait_ge(sem, n)
-        qu.dma_start(T.y[lo * R:hi * R, W * j:W * (j + 1)], T.land[K * j + lo:K * j + hi]).then_inc(S.stored, 16)
+        qu.dma_start(T.y[:, W * j:W * (j + 1)], T.land[K * j:K * (j + 1)]).then_inc(S.stored, 16)
 
-    store(g.sync, S.Ls, n_ls, left, 2, 4)
-    store(g.scalar, S.Rs, n_rs, right, 0, 2)
-    store(g.sync, S.Lr, 16, left, 0, 2)
-    store(g.scalar, S.Rr, 16, right, 2, 4)
-    store(g.sync, S.Da, 16, d, 0, 2)
-    store(g.scalar, S.Db, 16, d, 2, 4)
-    g.wait_ge(S.sent, 16)
-    g.dma_start(T.y[:, W * r:W * (r + 1)], T.x[:, :]).then_inc(S.own, 16)
-    g.wait_ge(S.own, 16)
-    g.wait_ge(S.stored, 96)
+    g.scalar.wait_ge(S.loaded, 16)
+    g.scalar.dma_start(T.y[:, W * q:W * (q + 1)], T.x[:, :]).then_inc(S.stored, 16)
+    store(g.sync, S.Sw, 16, sw)
+    store(g.scalar, S.Cb, 32, cb)
+    store(g.sync, S.D, 32, d)
+    g.wait_ge(S.sent, 14)
+    g.wait_ge(S.stored, 64)

@@ -1,21 +1,22 @@
 from concourse.bass import DstId, RemoteDMATransfer
 
 W = 256
-K = 4
+K = 8
 R = 128 // K
 SCRATCH = {'land': ('dram', [4 * K, 128, W // K], 'float32')}
-SEMAPHORES = ['loaded', 'sent', 'relay', 'spread', 'Sw', 'Cb', 'D', 'stored']
+SEMAPHORES = ['loaded', 'sent', 'relay', 'spread', 'Sw', 'Cb0', 'Cb1', 'D0', 'D1', 'stored']
 SENDER = (0, 4, 2, 6)
-RELAY = (1, 5, 3, 7)
+EXIT = (1, 5, 3, 7) + SENDER
 
 
 def rank_program(g, core, T, topo):
     S = T.sem
+    Cb, D = [S.Cb0, S.Cb1], [S.D0, S.D1]
 
-    def tr(j, c, dst, mask, sem):
+    def tr(j, s, dst, mask, sem):
         rid, pid = topo.addr(dst, core)
         return RemoteDMATransfer(dst_ids=[DstId(rid=rid, pnc=pid)], dma_engine_mask=mask, remote_sem=sem,
-                                 src=T.land[K * j + c], dst=T.land[K * j + c])
+                                 src=T.land[K * j + s], dst=T.land[K * j + s])
 
     q = T.rank_of(core - core % 8)
     if q is None:
@@ -23,39 +24,53 @@ def rank_program(g, core, T, topo):
     sw, cb, d = q ^ 1, 3 - q, (q + 2) % 4
     me = core % 8
 
-    def send_out(c):
-        g.remote_dma_fused([tr(q, c, T.cores[cb] + RELAY[c], 0x000F, S.relay),
-                            tr(q, c, T.cores[sw], 0x00F0, S.Sw)], local_sem=S.sent)
+    def out(s, m_cable, m_switch):
+        return [tr(q, s, T.cores[cb] + EXIT[s], m_cable, S.relay), tr(q, s, T.cores[sw], m_switch, S.Sw)]
+
+    def forward(s):
+        ts = [tr(cb, s, T.cores[sw], 0x00FF, D[s // 4])]
+        if me != 0:
+            ts.append(tr(cb, s, T.cores[q], 0xFF00, Cb[s // 4]))
+        g.remote_dma_fused(ts, local_sem=S.sent)
 
     if me != 0:
+        n = 16
         if me in SENDER:
-            g.wait_ge(S.spread, 2)
-            send_out(SENDER.index(me))
-            g.wait_ge(S.sent, 8)
-        else:
-            c = RELAY.index(me)
-            g.wait_ge(S.relay, 4)
-            g.remote_dma_fused([tr(cb, c, T.cores[sw], 0x00FF, S.D),
-                                tr(cb, c, T.cores[q], 0xFF00, S.Cb)], local_sem=S.sent)
-            g.wait_ge(S.sent, 16)
+            c = SENDER.index(me)
+            g.wait_ge(S.spread, 4)
+            g.remote_dma_fused(out(c, 0x000F, 0x00F0), local_sem=S.sent)
+            g.remote_dma_fused(out(c + 4, 0x000F, 0x00F0), local_sem=S.sent)
+            n += 16
+        s = EXIT.index(me)
+        g.wait_ge(S.relay, 2 if s % 4 == 0 else 4)
+        forward(s)
+        g.wait_ge(S.sent, n)
         return
 
     g.sync.dma_start(T.land[K * q:K * (q + 1)], T.x[:, :]).then_inc(S.loaded, 16)
     g.wait_ge(S.loaded, 16)
-    g.remote_dma_fused([tr(q, 0, T.cores[cb] + RELAY[0], 0x000F, S.relay),
-                        tr(q, 0, T.cores[sw], 0x00F0, S.Sw),
-                        tr(q, 1, core + SENDER[1], 0x0300, S.spread),
-                        tr(q, 2, core + SENDER[2], 0x0C00, S.spread),
-                        tr(q, 3, core + SENDER[3], 0x3000, S.spread)], local_sem=S.sent)
+    g.remote_dma_fused(out(0, 0x0003, 0x000C) + [
+        tr(q, s, core + SENDER[s % 4], 0x0030 << (2 * i), S.spread) for i, s in enumerate((1, 2, 3, 5, 6, 7))],
+        local_sem=S.sent)
+    g.remote_dma_fused(out(4, 0x0003, 0x000C), local_sem=S.sent)
+    g.wait_ge(S.relay, 2)
+    forward(4)
 
-    def store(qu, sem, n, j):
-        qu.wait_ge(sem, n)
-        qu.dma_start(T.y[:, W * j:W * (j + 1)], T.land[K * j:K * (j + 1)]).then_inc(S.stored, 16)
+    def store(qu, j, lo, hi):
+        qu.dma_start(T.y[lo * R:hi * R, W * j:W * (j + 1)], T.land[K * j + lo:K * j + hi]).then_inc(S.stored, 16)
 
     g.scalar.wait_ge(S.loaded, 16)
     g.scalar.dma_start(T.y[:, W * q:W * (q + 1)], T.x[:, :]).then_inc(S.stored, 16)
-    store(g.sync, S.Sw, 16, sw)
-    store(g.scalar, S.Cb, 32, cb)
-    store(g.sync, S.D, 32, d)
-    g.wait_ge(S.sent, 14)
-    g.wait_ge(S.stored, 64)
+    g.sync.wait_ge(S.Sw, 28)
+    store(g.sync, sw, 0, 8)
+    g.scalar.wait_ge(S.Cb0, 32)
+    store(g.scalar, cb, 0, 4)
+    g.sync.wait_ge(S.D0, 32)
+    store(g.sync, d, 0, 4)
+    g.scalar.wait_ge(S.Cb1, 24)
+    g.scalar.wait_ge(S.relay, 2)
+    store(g.scalar, cb, 4, 8)
+    g.sync.wait_ge(S.D1, 32)
+    store(g.sync, d, 4, 8)
+    g.wait_ge(S.sent, 28)
+    g.wait_ge(S.stored, 96)

@@ -1,22 +1,26 @@
 from concourse.bass import DstId, RemoteDMATransfer
 
 W = 256
-K = 8
-R = 128 // K
-SCRATCH = {'land': ('dram', [4 * K, 128, W // K], 'float32')}
-SEMAPHORES = ['loaded', 'sent', 'relay', 'spread', 'Sw', 'Cb0', 'Cb1', 'D0', 'D1', 'stored']
+RA, RB = 24, 8
+NA = 4 * RA
+SCRATCH = {'landA': ('dram', [16, 128, 2 * RA], 'float32'), 'landB': ('dram', [16, 128, 2 * RB], 'float32')}
+SEMAPHORES = ['loadedA', 'loadedB', 'sent', 'relay', 'spreadA', 'spreadB',
+              'SwA', 'SwB', 'CbA', 'CbB', 'DA', 'DB', 'stored']
 SENDER = (0, 4, 2, 6)
-EXIT = (1, 5, 3, 7) + SENDER
+EXIT_A = (1, 5, 3, 7)
+EXIT_B = SENDER
 
 
 def rank_program(g, core, T, topo):
     S = T.sem
-    Cb, D = [S.Cb0, S.Cb1], [S.D0, S.D1]
+    land = [T.landA, T.landB]
+    exits, spread = [EXIT_A, EXIT_B], [S.spreadA, S.spreadB]
+    Sw, Cb, D = [S.SwA, S.SwB], [S.CbA, S.CbB], [S.DA, S.DB]
 
-    def tr(j, s, dst, mask, sem):
+    def tr(w, j, c, dst, mask, sem):
         rid, pid = topo.addr(dst, core)
         return RemoteDMATransfer(dst_ids=[DstId(rid=rid, pnc=pid)], dma_engine_mask=mask, remote_sem=sem,
-                                 src=T.land[K * j + s], dst=T.land[K * j + s])
+                                 src=land[w][4 * j + c], dst=land[w][4 * j + c])
 
     q = T.rank_of(core - core % 8)
     if q is None:
@@ -24,53 +28,58 @@ def rank_program(g, core, T, topo):
     sw, cb, d = q ^ 1, 3 - q, (q + 2) % 4
     me = core % 8
 
-    def out(s, m_cable, m_switch):
-        return [tr(q, s, T.cores[cb] + EXIT[s], m_cable, S.relay), tr(q, s, T.cores[sw], m_switch, S.Sw)]
+    def out(w, c, m_cable, m_switch):
+        return [tr(w, q, c, T.cores[cb] + exits[w][c], m_cable, S.relay), tr(w, q, c, T.cores[sw], m_switch, Sw[w])]
 
-    def forward(s):
-        ts = [tr(cb, s, T.cores[sw], 0x00FF, D[s // 4])]
+    def forward(w, c):
+        ts = [tr(w, cb, c, T.cores[sw], 0x00FF, D[w])]
         if me != 0:
-            ts.append(tr(cb, s, T.cores[q], 0xFF00, Cb[s // 4]))
+            ts.append(tr(w, cb, c, T.cores[q], 0xFF00, Cb[w]))
         g.remote_dma_fused(ts, local_sem=S.sent)
 
     if me != 0:
-        n = 16
         if me in SENDER:
             c = SENDER.index(me)
-            g.wait_ge(S.spread, 4)
-            g.remote_dma_fused(out(c, 0x000F, 0x00F0), local_sem=S.sent)
-            g.remote_dma_fused(out(c + 4, 0x000F, 0x00F0), local_sem=S.sent)
-            n += 16
-        s = EXIT.index(me)
-        g.wait_ge(S.relay, 2 if s % 4 == 0 else 4)
-        forward(s)
-        g.wait_ge(S.sent, n)
+            for w in range(2):
+                g.wait_ge(spread[w], 4)
+                g.remote_dma_fused(out(w, c, 0x000F, 0x00F0), local_sem=S.sent)
+            g.wait_ge(S.relay, 4)
+            forward(1, c)
+            g.wait_ge(S.sent, 32)
+        else:
+            c = EXIT_A.index(me)
+            g.wait_ge(S.relay, 2 if c == 0 else 4)
+            forward(0, c)
+            g.wait_ge(S.sent, 16)
         return
 
-    g.sync.dma_start(T.land[K * q:K * (q + 1)], T.x[:, :]).then_inc(S.loaded, 16)
-    g.wait_ge(S.loaded, 16)
-    g.remote_dma_fused(out(0, 0x0003, 0x000C) + [
-        tr(q, s, core + SENDER[s % 4], 0x0030 << (2 * i), S.spread) for i, s in enumerate((1, 2, 3, 5, 6, 7))],
-        local_sem=S.sent)
-    g.remote_dma_fused(out(4, 0x0003, 0x000C), local_sem=S.sent)
+    g.sync.dma_start(T.landA[4 * q:4 * q + 4], T.x[0:NA, :]).then_inc(S.loadedA, 16)
+    g.scalar.dma_start(T.landB[4 * q:4 * q + 4], T.x[NA:128, :]).then_inc(S.loadedB, 16)
+    for w, sem in enumerate((S.loadedA, S.loadedB)):
+        g.wait_ge(sem, 16)
+        g.remote_dma_fused(out(w, 0, 0x0003, 0x000C) + [
+            tr(w, q, c, core + SENDER[c], 0x000F << (4 * c), spread[w]) for c in (1, 2, 3)], local_sem=S.sent)
     g.wait_ge(S.relay, 2)
-    forward(4)
+    forward(1, 0)
 
-    def store(qu, j, lo, hi):
-        qu.dma_start(T.y[lo * R:hi * R, W * j:W * (j + 1)], T.land[K * j + lo:K * j + hi]).then_inc(S.stored, 16)
+    def store(qu, w, j):
+        lo, hi = (0, NA) if w == 0 else (NA, 128)
+        qu.dma_start(T.y[lo:hi, W * j:W * (j + 1)], land[w][4 * j:4 * j + 4]).then_inc(S.stored, 16)
 
-    g.scalar.wait_ge(S.loaded, 16)
+    g.scalar.wait_ge(S.loadedA, 16)
     g.scalar.dma_start(T.y[:, W * q:W * (q + 1)], T.x[:, :]).then_inc(S.stored, 16)
-    g.sync.wait_ge(S.Sw, 28)
-    store(g.sync, sw, 0, 8)
-    g.scalar.wait_ge(S.Cb0, 32)
-    store(g.scalar, cb, 0, 4)
-    g.sync.wait_ge(S.D0, 32)
-    store(g.sync, d, 0, 4)
-    g.scalar.wait_ge(S.Cb1, 24)
+    g.sync.wait_ge(S.SwA, 14)
+    store(g.sync, 0, sw)
+    g.sync.wait_ge(S.SwB, 14)
+    store(g.sync, 1, sw)
+    g.scalar.wait_ge(S.CbA, 32)
+    store(g.scalar, 0, cb)
+    g.sync.wait_ge(S.DA, 32)
+    store(g.sync, 0, d)
+    g.scalar.wait_ge(S.CbB, 24)
     g.scalar.wait_ge(S.relay, 2)
-    store(g.scalar, cb, 4, 8)
-    g.sync.wait_ge(S.D1, 32)
-    store(g.sync, d, 4, 8)
-    g.wait_ge(S.sent, 28)
-    g.wait_ge(S.stored, 96)
+    store(g.scalar, 1, cb)
+    g.sync.wait_ge(S.DB, 32)
+    store(g.sync, 1, d)
+    g.wait_ge(S.sent, 40)
+    g.wait_ge(S.stored, 112)

from concourse.bass import DstId, RemoteDMATransfer

W = 256
RA, RB = 24, 8
NA = 4 * RA
SCRATCH = {'landA': ('dram', [16, 128, 2 * RA], 'float32'), 'landB': ('dram', [16, 128, 2 * RB], 'float32')}
SEMAPHORES = ['loadedA', 'loadedB', 'sent', 'relay', 'spreadA', 'spreadB',
              'SwA', 'SwB', 'CbA', 'CbB', 'DA', 'DB', 'stored']
SENDER = (0, 4, 2, 6)
EXIT_A = (1, 5, 3, 7)
EXIT_B = SENDER


def rank_program(g, core, T, topo):
    S = T.sem
    land = [T.landA, T.landB]
    exits, spread = [EXIT_A, EXIT_B], [S.spreadA, S.spreadB]
    Sw, Cb, D = [S.SwA, S.SwB], [S.CbA, S.CbB], [S.DA, S.DB]

    def tr(w, j, c, dst, mask, sem):
        rid, pid = topo.addr(dst, core)
        return RemoteDMATransfer(dst_ids=[DstId(rid=rid, pnc=pid)], dma_engine_mask=mask, remote_sem=sem,
                                 src=land[w][4 * j + c], dst=land[w][4 * j + c])

    q = T.rank_of(core - core % 8)
    if q is None:
        return
    sw, cb, d = q ^ 1, 3 - q, (q + 2) % 4
    me = core % 8

    def out(w, c, m_cable, m_switch):
        return [tr(w, q, c, T.cores[cb] + exits[w][c], m_cable, S.relay), tr(w, q, c, T.cores[sw], m_switch, Sw[w])]

    def forward(w, c):
        ts = [tr(w, cb, c, T.cores[sw], 0x00FF, D[w])]
        if me != 0:
            ts.append(tr(w, cb, c, T.cores[q], 0xFF00, Cb[w]))
        g.remote_dma_fused(ts, local_sem=S.sent)

    if me != 0:
        if me in SENDER:
            c = SENDER.index(me)
            for w in range(2):
                g.wait_ge(spread[w], 4)
                g.remote_dma_fused(out(w, c, 0x000F, 0x00F0), local_sem=S.sent)
            g.wait_ge(S.relay, 4)
            forward(1, c)
            g.wait_ge(S.sent, 32)
        else:
            c = EXIT_A.index(me)
            g.wait_ge(S.relay, 2 if c == 0 else 4)
            forward(0, c)
            g.wait_ge(S.sent, 16)
        return

    g.sync.dma_start(T.landA[4 * q:4 * q + 4], T.x[0:NA, :]).then_inc(S.loadedA, 16)
    g.scalar.dma_start(T.landB[4 * q:4 * q + 4], T.x[NA:128, :]).then_inc(S.loadedB, 16)
    for w, sem in enumerate((S.loadedA, S.loadedB)):
        g.wait_ge(sem, 16)
        g.remote_dma_fused(out(w, 0, 0x0003, 0x000C) + [
            tr(w, q, c, core + SENDER[c], 0x000F << (4 * c), spread[w]) for c in (1, 2, 3)], local_sem=S.sent)
    g.wait_ge(S.relay, 2)
    forward(1, 0)

    def store(qu, w, j):
        lo, hi = (0, NA) if w == 0 else (NA, 128)
        qu.dma_start(T.y[lo:hi, W * j:W * (j + 1)], land[w][4 * j:4 * j + 4]).then_inc(S.stored, 16)

    g.scalar.wait_ge(S.loadedA, 16)
    g.scalar.dma_start(T.y[:, W * q:W * (q + 1)], T.x[:, :]).then_inc(S.stored, 16)
    g.sync.wait_ge(S.SwA, 14)
    store(g.sync, 0, sw)
    g.sync.wait_ge(S.SwB, 14)
    store(g.sync, 1, sw)
    g.scalar.wait_ge(S.CbA, 32)
    store(g.scalar, 0, cb)
    g.sync.wait_ge(S.DA, 32)
    store(g.sync, 0, d)
    g.scalar.wait_ge(S.CbB, 24)
    g.scalar.wait_ge(S.relay, 2)
    store(g.scalar, 1, cb)
    g.sync.wait_ge(S.DB, 32)
    store(g.sync, 1, d)
    g.wait_ge(S.sent, 40)
    g.wait_ge(S.stored, 112)
